import numpy as np
import ml_dtypes


def mxq(x, axis, fmt="e4m3"):
    dtype, down = {"e4m3": (ml_dtypes.float8_e4m3fn, 7), "e5m2": (ml_dtypes.float8_e5m2, 14)}[fmt]
    v = np.moveaxis(np.asarray(x, np.float32).astype(ml_dtypes.bfloat16).astype(np.float64), axis, -1)
    blocks = v.reshape(v.shape[:-1] + (-1, 32))
    amax = np.abs(blocks).max(-1, keepdims=True)
    byte = np.maximum(np.where(amax > 0, np.frexp(amax)[1] - 1 + 127, 0) - down, 1)
    scale = np.exp2(byte - 127.0)
    codes = (blocks / scale).astype(np.float32).astype(dtype).astype(np.float64)
    return np.moveaxis((codes * scale).reshape(v.shape), -1, axis)


WIDE = False


def mx_kscale(k):
    if not WIDE:
        return np.ones(k)
    levels = np.array([10, -10, 5, -5, 0])
    if k % 512:
        return np.exp2(np.random.permutation(np.resize(levels, k // 32))).repeat(32)
    a = np.empty((k // 512, 16))
    for p in range(k // 512):
        a[p, :8] = np.random.permutation(np.resize(levels, 8))
        for g in range(8):
            far = levels[np.abs(levels - a[p, g]) >= 10]
            a[p, g + 8] = far[np.random.randint(len(far))]
    return np.exp2(a.ravel()).repeat(32)


def f64(x):
    return np.asarray(x).astype(np.float64)


def striped(idx):
    return np.tile(idx.reshape(-1, 16).T, (8, 1)).astype(np.uint16)


def unstriped(offs):
    return offs[:16].T.reshape(-1).astype(np.int64)


def striped8(idx):
    return np.concatenate([x.reshape(-1, 16).T for x in idx]).astype(np.uint16)


def runs(offs, k):
    lists = np.stack([offs[16 * r : 16 * r + 16].T.reshape(-1) for r in range(8)]).astype(np.int64)
    return lists[np.arange(k) % 512 // 64]


def pack_weight(w):
    k, n = w.shape
    w = f64(np.asarray(w, np.float32).astype(ml_dtypes.bfloat16)).reshape(k // 32, 32, n)
    amax = np.abs(w).max(1)
    byte = np.clip(np.where(amax > 0, np.frexp(amax)[1] - 1 + 127 - 7, 1), 1, 254)
    scaled = (w * np.exp2(127.0 - byte)[:, None, :]).reshape(k, n).astype(np.float32)
    words = np.ascontiguousarray(scaled.reshape(k // 512, 128, 4, n).transpose(0, 1, 3, 2)).astype(ml_dtypes.float8_e4m3fn).view(np.uint8)
    return words, np.ascontiguousarray(byte.astype(np.uint8).reshape(k // 512, 16, n))


def unpack_weight(words, scales):
    g, p, n, _ = words.shape
    vals = np.ascontiguousarray(words).view(ml_dtypes.float8_e4m3fn).astype(np.float64) * np.repeat(np.exp2(scales.astype(np.float64) - 127.0), 8, axis=1)[..., None]
    return vals.transpose(0, 1, 3, 2).reshape(g * 512, n)


K, T, S, N, H, W, C = 512, 2048, 512, 512, 512, 384, 512


def setup_inputs():
    n = np.random.standard_normal
    s = mx_kscale(K)[:, None]
    u = mx_kscale(S)
    packed_xT = pack_weight(n((K, T)) * s)
    return {
        "x_words": packed_xT[0],
        "x_scales": packed_xT[1],
        "w1": (n((K, H)) / np.sqrt(K) / s).astype(np.float32),
        "w2": (n((K, H)) / np.sqrt(K) / s).astype(np.float32),
        "gn": (np.random.uniform(0.5, 1.5, (H, 1)) * u[:, None]).astype(np.float32),
        "w3": (n((H, N)) / np.sqrt(H) / u[:, None]).astype(np.float32),
        "gs": (np.random.uniform(0.5, 1.5, (K, 1)) / s).astype(np.float32),
        "offs": striped(np.random.permutation(T)[:S]),
        "two": striped(np.random.permutation(T)[:S]),
        "n1": striped8(np.stack([np.random.permutation(S) for _ in range(8)])),
        "n2": striped(np.random.permutation(S)[:W]),
        "n3": striped(np.random.permutation(S)[:W]),
        "cand": striped(np.random.permutation(T)[:C]),
        "n4": striped(np.random.permutation(S)),
        "n5": striped(np.random.permutation(S)),
    }


def reference(x_words, x_scales, w1, w2, gn, w3, gs, offs, two, n1, n2, n3, cand, n4, n5):
    xq = unpack_weight(x_words, x_scales)[:, unstriped(offs)]
    y = mxq(f64(w1), 0, "e4m3").T @ xq
    z = f64(gn) * (y - (y[np.arange(H)[:, None], runs(n1, H)]))
    a = mxq(f64(w3), 0, "e4m3").T @ mxq(z, 0, "e4m3")
    x_cand = unpack_weight(x_words, x_scales)[:, unstriped(cand)]
    x_two = unpack_weight(x_words, x_scales)[:, unstriped(two)]
    d = mxq(f64(w2), 0, "e4m3").T @ x_two
    pa = d[:, unstriped(n3)]
    old = d[:, unstriped(n2)]
    ra = np.maximum(pa, 0.5 * old)
    ds = d.copy()
    ds[:, unstriped(n2)] = ra
    z2 = f64(gs) * ds
    b = 0.0625 * ((x_cand.T @ mxq(z2, 0, "e4m3")))
    return 0.75 * (a * b[:, unstriped(n5)] - (a[:, unstriped(n4)] * b))

@@ -1,0 +1,248 @@
+from contextlib import ExitStack
+
+import concourse.mybir as mybir
+
+K, T, S, N, H, W, C = 512, 2048, 512, 512, 512, 384, 512
+FLOPS = 4 * 2 * 512 * 512 * 512
+
+F32 = mybir.dt.float32
+BF16 = mybir.dt.bfloat16
+I32 = mybir.dt.int32
+U32 = mybir.dt.uint32
+U16 = mybir.dt.uint16
+U8 = mybir.dt.uint8
+FP8X4 = mybir.dt.float8_e4m3fn_x4
+ALU = mybir.AluOpType
+COPY = mybir.ActivationFunctionType.Copy
+
+P = 128
+PACK = 4
+HALF = 256
+SPARE = 32
+OUT_SCALE = 0.75 * 0.0625
+
+
+def tile_picked_tfcdcrossbdifkmax_none_p_kernel(
+    tc, x_words, x_scales, w1, w2, gn, w3, gs, offs, two, n1, n2, n3, cand, n4, n5, out
+):
+    nc = tc.nc
+    with ExitStack() as ctx:
+        lists = ctx.enter_context(tc.tile_pool(name="lists", bufs=1))
+        sb = ctx.enter_context(tc.tile_pool(name="sb", bufs=1))
+        ps = ctx.enter_context(tc.psum_pool(name="ps", bufs=1))
+        halves = [slice(0, HALF), slice(HALF, 2 * HALF)]
+        whole = slice(0, 512)
+
+        def new(name, shape, dtype, on=None):
+            return sb.tile(shape, dtype, name=name, tag=on or name, align_bytes=64)
+
+        def four(name, width, dtype=F32):
+            return [new("%s%d" % (name, t), [P, width], dtype) for t in range(4)]
+
+        def load_list(name, ap):
+            tl = lists.tile(list(ap.shape), U16, name=name)
+            nc.sync.dma_start(tl[:], ap)
+            return tl
+
+        def load_weight(name, w, cols):
+            raw = new(name, [P, PACK, cols.stop - cols.start], F32)
+            nc.sync.dma_start(raw[:], w.rearrange("(p j) c -> p j c", j=PACK)[:, :, cols])
+            return raw
+
+        def load_gain(name, g):
+            tl = new(name, [P, PACK], F32)
+            nc.sync.dma_start(tl[:], g.rearrange("(p t) o -> p (t o)", t=PACK))
+            return tl
+
+        def codes(name, on=None):
+            return new(name + "_codes", [P, 512], U32, on)
+
+        def scales(name, on=None):
+            return new(name + "_scales", [P, 512], U8, on)
+
+        def mx(name):
+            return (codes(name), scales(name))
+
+        def grouped(name, on=None):
+            return new(name + "_grouped", [P, 512 * PACK], BF16, on)
+
+        def pick_bytes(dst, lst):
+            nc.vector.tensor_copy(dst[:], xs[:].indirect(lst[:]))
+
+        def pick_words(dst, lst):
+            nc.vector.tensor_copy(dst[:], xw[:].bitcast(U32).indirect(lst[:]))
+
+        def words4(cols):
+            return slice(PACK * cols.start, PACK * cols.stop)
+
+        def quantize(q, g, cols=whole):
+            nc.vector.quantize_mx(out=q[0][:, cols].bitcast(FP8X4), scales=q[1][:, cols], in_=g[:, words4(cols)])
+
+        def product(bank, lhs, t, rhs, cols=whole):
+            st = slice(P * t, P * (t + 1))
+            nc.tensor.matmul_mx(
+                out=bank[:, cols], lhsT=lhs[0][:, st].bitcast(FP8X4), lhsT_scale=lhs[1][:, st],
+                rhs=rhs[0][:, cols].bitcast(FP8X4), rhs_scale=rhs[1][:, cols], start=True, stop=True,
+            )
+
+        def pool_cast(dst, src):
+            nc.gpsimd.tensor_scalar(dst, src, 1.0, 0.0, ALU.mult, ALU.add)
+
+        def cp(eng):
+            return {"s": nc.scalar.copy, "v": nc.vector.tensor_copy, "g": pool_cast}[eng]
+
+        def deal_half(eng, g, raw, h):
+            dst = g[:].rearrange("p (t m j) -> p m j t", t=PACK, j=PACK)[:, 64 * h : 64 * (h + 1)]
+            cp(eng)(dst, raw[:].rearrange("p j (m t) -> p m j t", t=PACK))
+
+        def weave_out(g):
+            return g.rearrange("p (c i t) -> p c t i", i=4, t=PACK)
+
+        def weave_in(planes):
+            return planes.rearrange("p t (c i) -> p c t i", i=4)
+
+        def weave(eng, g, planes, cols):
+            cp(eng)(weave_out(g[:, words4(cols)]), weave_in(planes[:, :, cols]))
+
+        def gather(eng, dst, win, lst):
+            if eng == "s":
+                nc.scalar.activation(dst, win.indirect(lst), COPY)
+            else:
+                nc.vector.tensor_copy(dst, win.indirect(lst))
+
+        def scatter(eng, win, lst, src):
+            if eng == "s":
+                nc.scalar.activation(win.indirect(lst), src, COPY)
+            else:
+                nc.vector.tensor_copy(win.indirect(lst), src)
+
+        def banks(name, tag):
+            return [ps.tile([P, S], F32, name="%s%d" % (name, t), tag="%s%d" % (tag, t)) for t in range(4)]
+
+        def scaled(eng, dst, src, scale):
+            if eng == "s":
+                nc.scalar.activation(dst, src, COPY, scale=scale)
+            elif eng == "g":
+                nc.gpsimd.tensor_scalar(dst, src, scale, 0.0, ALU.mult, ALU.add)
+            else:
+                nc.vector.tensor_scalar(dst, src, scale, None, ALU.mult)
+
+        def larger(t):
+            nc.vector.scalar_tensor_tensor(ra[t][:], old[t][:], 0.5, pa[t][:], ALU.mult, ALU.max)
+
+        def weigh(eng, t):
+            scaled(eng, z2_planes[:, t, :], d_win[t][:], gs_t[:, t : t + 1])
+
+        def y_out(eng, t):
+            scaled(eng, y_win[t][:], y_ps[t][:], gn_t[:, t : t + 1])
+            nc.sync.dma_start(y_all[:, t, :], y_win[t][:])
+
+        def n1_gather(eng, t, h):
+            gather(eng, y_n1[:, t, halves[h]], y_win[t][:], n1_l[:, 16 * h : 16 * (h + 1)])
+
+        def z_half(h):
+            cols = halves[h]
+            nc.vector.tensor_tensor(weave_out(z_g[:, words4(cols)]), weave_in(y_all[:, :, cols]), weave_in(y_n1[:, :, cols]), ALU.subtract)
+
+        def finish(m, sub=nc.vector):
+            sub.tensor_tensor(res[m][:], left[m][:], right[m][:], ALU.subtract)
+            nc.sync.dma_start(out[P * m : P * (m + 1), :], res[m][:])
+
+        xs = new("xs", [P, T], U8)
+        nc.gpsimd.memset(xs[:].bitcast(I32), 0)
+        two_l = load_list("two_l", two)
+        offs_l = load_list("offs_l", offs)
+        for q in range(4):
+            nc.sync.dma_start(xs[32 * q : 32 * q + 4, :].bitcast(I32), x_scales[0, 4 * q : 4 * q + 4, :].bitcast(I32))
+        w2_raw = [load_weight("w2_raw%d" % h, w2, halves[h]) for h in range(2)]
+        cand_l = load_list("cand_l", cand)
+        xw = new("xw", [P, T], I32)
+        nc.sync.dma_start(xw[:], x_words[0].rearrange("p c r -> p (c r)").bitcast(I32))
+        n3_l = load_list("n3_l", n3)
+        n2_l = load_list("n2_l", n2)
+        w1_raw = [load_weight("w1_raw%d" % h, w1, halves[h]) for h in range(2)]
+        gs_t = load_gain("gs_t", gs)
+        gn_t = load_gain("gn_t", gn)
+        n1_l = load_list("n1_l", n1)
+        w3_raw = load_weight("w3_raw", w3, whole)
+        n5_l = load_list("n5_l", n5)
+        n4_l = load_list("n4_l", n4)
+        a_win, b_win = four("a_win", S + SPARE), four("b_win", S + SPARE)
+        for win in a_win + b_win:
+            nc.gpsimd.memset(win[:, S:], 0.0)
+        d_win, pa, old, ra = four("d_win", S), four("pa", W), four("old", W), four("ra", W)
+        y_win = four("y_win", S)
+        y_all = new("y_all", [P, PACK, S], F32)
+        y_n1 = new("y_n1", [P, PACK, S], F32)
+        b_n5, a_n4, left, right, res = [four(nm, S) for nm in ("b_n5_", "a_n4_", "left", "right", "res")]
+        x_two, x_offs = mx("x_two"), mx("x_offs")
+        w1_q, w2_q, w3_q, z_q, z2_q = [mx(nm) for nm in ("w1", "w2", "w3", "z", "z2")]
+        w1_g, w2_g, z_g, z2_g = [grouped(nm) for nm in ("w1", "w2", "z", "z2")]
+        z2_planes = new("z2_planes", [P, PACK, S], BF16)
+
+        x_cand = (codes("x_cand", on="old3"), scales("x_cand", on="w2_grouped"))
+        w3_g = grouped("w3", on="z2_planes")
+        pick_bytes(x_two[1], two_l)
+        pick_bytes(x_offs[1], offs_l)
+        deal_half("s", w2_g, w2_raw[0], 0)
+        deal_half("s", w2_g, w2_raw[1], 1)
+        quantize(w2_q, w2_g)
+        pick_words(x_two[0], two_l)
+        d_ps = banks("d_ps", "db")
+        for t in range(4):
+            product(d_ps[t], w2_q, t, x_two)
+        pick_bytes(x_cand[1], cand_l)
+        pick_words(x_offs[0], offs_l)
+        deal_half("s", w1_g, w1_raw[0], 0)
+        for t in range(4):
+            nc.scalar.copy(d_win[t][:], d_ps[t][:])
+            gather("s", pa[t][:], d_win[t][:], n3_l[:])
+            gather("v" if t == 0 else "s", old[t][:], d_win[t][:], n2_l[:])
+            larger(t)
+            if t == 0:
+                deal_half("v", w1_g, w1_raw[1], 1)
+                quantize(w1_q, w1_g)
+                y_ps = banks("y_ps", "ya")
+                for u in range(4):
+                    product(y_ps[u], w1_q, u, x_offs)
+            if t != 2:
+                scatter("v", d_win[t][:], n2_l[:], ra[t][:])
+        y_out("s", 0)
+        scatter("s", d_win[2][:], n2_l[:], ra[2][:])
+        pick_words(x_cand[0], cand_l)
+        for t in range(4):
+            weigh("v", t)
+        for t in range(1, 4):
+            y_out("s", t)
+        b_ps = banks("b_ps", "db")
+        for h in range(2):
+            weave("v", z2_g, z2_planes, halves[h])
+        for h in range(2):
+            quantize(z2_q, z2_g, halves[h])
+        for m in range(4):
+            product(b_ps[m], x_cand, m, z2_q)
+        for h in range(2):
+            weave("v", w3_g, w3_raw, halves[h])
+        quantize(w3_q, w3_g)
+        for h in range(2):
+            for t in range(4):
+                n1_gather("s", t, h)
+        for h in range(2):
+            z_half(h)
+        for h in range(2):
+            quantize(z_q, z_g, halves[h])
+        a_ps = banks("a_ps", "ya")
+        for m in range(4):
+            product(a_ps[m], w3_q, m, z_q)
+        for m in range(4):
+            scaled("s", b_win[m][:, 0:S], b_ps[m][:], OUT_SCALE)
+            gather("s", b_n5[m][:], b_win[m][:], n5_l[:])
+        for m in range(4):
+            cp("v" if m < 2 else "s")(a_win[m][:, 0:S], a_ps[m][:])
+            if m < 2:
+                nc.vector.tensor_tensor(right[m][:], a_win[m][:].indirect(n4_l[:]), b_win[m][:, 0:S], ALU.mult)
+            nc.vector.tensor_tensor(left[m][:], a_win[m][:, 0:S], b_n5[m][:], ALU.mult)
+            if m >= 2:
+                gather("s", a_n4[m][:], a_win[m][:], n4_l[:])
+                nc.vector.tensor_tensor(right[m][:], a_n4[m][:], b_win[m][:, 0:S], ALU.mult)
+            finish(m)

@@ -152,10 +152,10 @@ def tile_picked_tfcdcrossbdifkmax_none_p_kernel(
         nc.gpsimd.memset(xs[:].bitcast(I32), 0)
         two_l = load_list("two_l", two)
         offs_l = load_list("offs_l", offs)
+        cand_l = load_list("cand_l", cand)
         for q in range(4):
             nc.sync.dma_start(xs[32 * q : 32 * q + 4, :].bitcast(I32), x_scales[0, 4 * q : 4 * q + 4, :].bitcast(I32))
-        w2_raw = [load_weight("w2_raw%d" % h, w2, halves[h]) for h in range(2)]
-        cand_l = load_list("cand_l", cand)
+        w2_raw = load_weight("w2_raw", w2, whole)
         xw = new("xw", [P, T], I32)
         nc.sync.dma_start(xw[:], x_words[0].rearrange("p c r -> p (c r)").bitcast(I32))
         n3_l = load_list("n3_l", n3)
@@ -170,49 +170,60 @@ def tile_picked_tfcdcrossbdifkmax_none_p_kernel(
         a_win, b_win = four("a_win", S + SPARE), four("b_win", S + SPARE)
         for win in a_win + b_win:
             nc.gpsimd.memset(win[:, S:], 0.0)
-        d_win, pa, old, ra = four("d_win", S), four("pa", W), four("old", W), four("ra", W)
+        d_win = four("d_win", S)
+        pa, old, ra = [[new("%s%d" % (nm, u), [P, 2, W], F32) for u in range(2)] for nm in ("pa", "old", "ra")]
         y_win = four("y_win", S)
         y_all = new("y_all", [P, PACK, S], F32)
         y_n1 = new("y_n1", [P, PACK, S], F32)
         b_n5, a_n4, left, right, res = [four(nm, S) for nm in ("b_n5_", "a_n4_", "left", "right", "res")]
         x_two, x_offs = mx("x_two"), mx("x_offs")
-        w1_q, w2_q, w3_q, z_q, z2_q = [mx(nm) for nm in ("w1", "w2", "w3", "z", "z2")]
-        w1_g, w2_g, z_g, z2_g = [grouped(nm) for nm in ("w1", "w2", "z", "z2")]
-        z2_planes = new("z2_planes", [P, PACK, S], BF16)
+        w1_q, w2_q, z_q, z2_q = [mx(nm) for nm in ("w1", "w2", "z", "z2")]
+        w1_g, w2_g, z2_g = [grouped(nm) for nm in ("w1", "w2", "z2")]
+        z_g = grouped("z", on="z2_grouped")
+        w3_g = grouped("w3", on="old0")
+        z2_planes = new("z2_planes", [P, PACK, S], BF16, on="pa1")
+        w3_q = (codes("w3", on="pa1"), scales("w3"))
+        x_cand = (codes("x_cand", on="old1"), scales("x_cand"))
 
-        x_cand = (codes("x_cand", on="old3"), scales("x_cand", on="w2_grouped"))
-        w3_g = grouped("w3", on="z2_planes")
         pick_bytes(x_two[1], two_l)
         pick_bytes(x_offs[1], offs_l)
-        deal_half("s", w2_g, w2_raw[0], 0)
-        deal_half("s", w2_g, w2_raw[1], 1)
+        pick_bytes(x_cand[1], cand_l)
+        deal_half("s", w2_g, w2_raw[:, :, halves[0]], 0)
+        deal_half("g", w2_g, w2_raw[:, :, halves[1]], 1)
         quantize(w2_q, w2_g)
         pick_words(x_two[0], two_l)
         d_ps = banks("d_ps", "db")
         for t in range(4):
             product(d_ps[t], w2_q, t, x_two)
-        pick_bytes(x_cand[1], cand_l)
         pick_words(x_offs[0], offs_l)
-        deal_half("s", w1_g, w1_raw[0], 0)
-        for t in range(4):
-            nc.scalar.copy(d_win[t][:], d_ps[t][:])
-            gather("s", pa[t][:], d_win[t][:], n3_l[:])
-            gather("v" if t == 0 else "s", old[t][:], d_win[t][:], n2_l[:])
-            larger(t)
-            if t == 0:
-                deal_half("v", w1_g, w1_raw[1], 1)
+        deal_half("g", w1_g, w1_raw[0], 0)
+        deal_half("g", w1_g, w1_raw[1], 1)
+        y_ps = banks("y_ps", "ya")
+        for u in range(2):
+            for e, eng in enumerate("vs"):
+                t = 2 * u + e
+                nc.scalar.copy(d_win[t][:], d_ps[t][:])
+            for e, eng in enumerate("vs"):
+                t = 2 * u + e
+                gather(eng, pa[u][:, e, :], d_win[t][:], n3_l[:])
+                gather(eng, old[u][:, e, :], d_win[t][:], n2_l[:])
+            if u == 0:
                 quantize(w1_q, w1_g)
-                y_ps = banks("y_ps", "ya")
-                for u in range(4):
-                    product(y_ps[u], w1_q, u, x_offs)
-            if t != 2:
-                scatter("v", d_win[t][:], n2_l[:], ra[t][:])
-        y_out("s", 0)
-        scatter("s", d_win[2][:], n2_l[:], ra[2][:])
+                for t in range(4):
+                    product(y_ps[t], w1_q, t, x_offs)
+            larger(u)
+            if u == 1:
+                y_out("s", 0)
+                y_out("s", 1)
+            for e, eng in enumerate("vs"):
+                scatter(eng, d_win[2 * u + e][:], n2_l[:], ra[u][:, e, :])
+            if u == 0:
+                for h in range(2):
+                    weave("g", w3_g, w3_raw, halves[h])
         pick_words(x_cand[0], cand_l)
         for t in range(4):
-            weigh("v", t)
-        for t in range(1, 4):
+            weigh("gggg"[t], t)
+        for t in range(2, 4):
             y_out("s", t)
         b_ps = banks("b_ps", "db")
         for h in range(2):
@@ -221,28 +232,30 @@ def tile_picked_tfcdcrossbdifkmax_none_p_kernel(
             quantize(z2_q, z2_g, halves[h])
         for m in range(4):
             product(b_ps[m], x_cand, m, z2_q)
-        for h in range(2):
-            weave("v", w3_g, w3_raw, halves[h])
         quantize(w3_q, w3_g)
         for h in range(2):
             for t in range(4):
-                n1_gather("s", t, h)
+                n1_gather("sssvssss"[4 * h + t], t, h)
+        a_ps = banks("a_ps", "ya")
         for h in range(2):
             z_half(h)
-        for h in range(2):
             quantize(z_q, z_g, halves[h])
-        a_ps = banks("a_ps", "ya")
         for m in range(4):
             product(a_ps[m], w3_q, m, z_q)
+
+        def list_halves(eng, dst, win, lst):
+            if eng == "s":
+                gather("s", dst[:], win[:], lst[:])
+            else:
+                for h in range(2):
+                    gather("v" if eng == "v" else "vs"[h], dst[:, halves[h]], win[:], lst[:, 16 * h : 16 * (h + 1)])
+
         for m in range(4):
-            scaled("s", b_win[m][:, 0:S], b_ps[m][:], OUT_SCALE)
-            gather("s", b_n5[m][:], b_win[m][:], n5_l[:])
+            scaled("ssss"[m], b_win[m][:, 0:S], b_ps[m][:], OUT_SCALE)
+            list_halves("ssss"[m], b_n5[m], b_win[m], n5_l)
         for m in range(4):
-            cp("v" if m < 2 else "s")(a_win[m][:, 0:S], a_ps[m][:])
-            if m < 2:
-                nc.vector.tensor_tensor(right[m][:], a_win[m][:].indirect(n4_l[:]), b_win[m][:, 0:S], ALU.mult)
-            nc.vector.tensor_tensor(left[m][:], a_win[m][:, 0:S], b_n5[m][:], ALU.mult)
-            if m >= 2:
-                gather("s", a_n4[m][:], a_win[m][:], n4_l[:])
-                nc.vector.tensor_tensor(right[m][:], a_n4[m][:], b_win[m][:, 0:S], ALU.mult)
-            finish(m)
+            cp("vvss"[m])(a_win[m][:, 0:S], a_ps[m][:])
+            list_halves("vvss"[m], a_n4[m], a_win[m], n4_l)
+            nc.vector.tensor_tensor(left[m][:], a_ps[m][:], b_n5[m][:], ALU.mult)
+            nc.vector.scalar_tensor_tensor(right[m][:], b_ps[m][:], OUT_SCALE, a_n4[m][:], ALU.mult, ALU.mult)
+            finish(m, nc.gpsimd if "gggv"[m] == "g" else nc.vector)

@@ -138,11 +138,11 @@ def tile_picked_tfcdcrossbdifkmax_none_p_kernel(
             nc.sync.dma_start(y_all[:, t, :], y_win[t][:])
 
         def n1_gather(eng, t, h):
-            gather(eng, y_n1[:, t, halves[h]], y_win[t][:], n1_l[:, 16 * h : 16 * (h + 1)])
+            gather(eng, y_n1[h][:, t, :], y_win[t][:], n1_l[:, 16 * h : 16 * (h + 1)])
 
         def z_half(h):
             cols = halves[h]
-            nc.vector.tensor_tensor(weave_out(z_g[:, words4(cols)]), weave_in(y_all[:, :, cols]), weave_in(y_n1[:, :, cols]), ALU.subtract)
+            nc.vector.tensor_tensor(weave_out(z_g[:, words4(cols)]), weave_in(y_all[:, :, cols]), weave_in(y_n1[h][:]), ALU.subtract)
 
         def finish(m, sub=nc.vector):
             sub.tensor_tensor(res[m][:], left[m][:], right[m][:], ALU.subtract)
@@ -151,13 +151,14 @@ def tile_picked_tfcdcrossbdifkmax_none_p_kernel(
         xs = new("xs", [P, T], U8)
         nc.gpsimd.memset(xs[:].bitcast(I32), 0)
         two_l = load_list("two_l", two)
+        w2_raw = [load_weight("w2_raw0", w2, halves[0])]
         offs_l = load_list("offs_l", offs)
-        cand_l = load_list("cand_l", cand)
         for q in range(4):
             nc.sync.dma_start(xs[32 * q : 32 * q + 4, :].bitcast(I32), x_scales[0, 4 * q : 4 * q + 4, :].bitcast(I32))
-        w2_raw = load_weight("w2_raw", w2, whole)
+        w2_raw.append(load_weight("w2_raw1", w2, halves[1]))
         xw = new("xw", [P, T], I32)
         nc.sync.dma_start(xw[:], x_words[0].rearrange("p c r -> p (c r)").bitcast(I32))
+        cand_l = load_list("cand_l", cand)
         n3_l = load_list("n3_l", n3)
         n2_l = load_list("n2_l", n2)
         w1_raw = [load_weight("w1_raw%d" % h, w1, halves[h]) for h in range(2)]
@@ -168,34 +169,34 @@ def tile_picked_tfcdcrossbdifkmax_none_p_kernel(
         n5_l = load_list("n5_l", n5)
         n4_l = load_list("n4_l", n4)
         a_win, b_win = four("a_win", S + SPARE), four("b_win", S + SPARE)
-        for win in a_win + b_win:
+        for win in a_win + b_win[1:]:
             nc.gpsimd.memset(win[:, S:], 0.0)
         d_win = four("d_win", S)
         pa, old, ra = [[new("%s%d" % (nm, u), [P, 2, W], F32) for u in range(2)] for nm in ("pa", "old", "ra")]
         y_win = four("y_win", S)
         y_all = new("y_all", [P, PACK, S], F32)
-        y_n1 = new("y_n1", [P, PACK, S], F32)
+        y_n1 = [new("y_n1_%d" % h, [P, PACK, HALF], F32) for h in range(2)]
         b_n5, a_n4, left, right, res = [four(nm, S) for nm in ("b_n5_", "a_n4_", "left", "right", "res")]
         x_two, x_offs = mx("x_two"), mx("x_offs")
         w1_q, w2_q, z_q, z2_q = [mx(nm) for nm in ("w1", "w2", "z", "z2")]
         w1_g, w2_g, z2_g = [grouped(nm) for nm in ("w1", "w2", "z2")]
         z_g = grouped("z", on="z2_grouped")
-        w3_g = grouped("w3", on="old0")
-        z2_planes = new("z2_planes", [P, PACK, S], BF16, on="pa1")
-        w3_q = (codes("w3", on="pa1"), scales("w3"))
+        w3_g = [new("w3_g%d" % h, [P, HALF * PACK], BF16, on="pa%d" % h) for h in range(2)]
+        z2_planes = new("z2_planes", [P, PACK, S], BF16)
+        w3_q = (codes("w3", on="z2_planes"), scales("w3"))
         x_cand = (codes("x_cand", on="old1"), scales("x_cand"))
 
         pick_bytes(x_two[1], two_l)
         pick_bytes(x_offs[1], offs_l)
-        pick_bytes(x_cand[1], cand_l)
-        deal_half("s", w2_g, w2_raw[:, :, halves[0]], 0)
-        deal_half("g", w2_g, w2_raw[:, :, halves[1]], 1)
+        deal_half("s", w2_g, w2_raw[0], 0)
+        deal_half("s", w2_g, w2_raw[1], 1)
         quantize(w2_q, w2_g)
         pick_words(x_two[0], two_l)
         d_ps = banks("d_ps", "db")
         for t in range(4):
             product(d_ps[t], w2_q, t, x_two)
         pick_words(x_offs[0], offs_l)
+        pick_bytes(x_cand[1], cand_l)
         deal_half("g", w1_g, w1_raw[0], 0)
         deal_half("g", w1_g, w1_raw[1], 1)
         y_ps = banks("y_ps", "ya")
@@ -205,8 +206,8 @@ def tile_picked_tfcdcrossbdifkmax_none_p_kernel(
                 nc.scalar.copy(d_win[t][:], d_ps[t][:])
             for e, eng in enumerate("vs"):
                 t = 2 * u + e
-                gather(eng, pa[u][:, e, :], d_win[t][:], n3_l[:])
-                gather(eng, old[u][:, e, :], d_win[t][:], n2_l[:])
+                gather("vvssvvss"[2 * t], pa[u][:, e, :], d_win[t][:], n3_l[:])
+                gather("vvssvvss"[2 * t + 1], old[u][:, e, :], d_win[t][:], n2_l[:])
             if u == 0:
                 quantize(w1_q, w1_g)
                 for t in range(4):
@@ -217,12 +218,10 @@ def tile_picked_tfcdcrossbdifkmax_none_p_kernel(
                 y_out("s", 1)
             for e, eng in enumerate("vs"):
                 scatter(eng, d_win[2 * u + e][:], n2_l[:], ra[u][:, e, :])
-            if u == 0:
-                for h in range(2):
-                    weave("g", w3_g, w3_raw, halves[h])
+            cp("g")(weave_out(w3_g[u][:]), weave_in(w3_raw[:, :, halves[u]]))
         pick_words(x_cand[0], cand_l)
         for t in range(4):
-            weigh("gggg"[t], t)
+            weigh("vvvv"[t], t)
         for t in range(2, 4):
             y_out("s", t)
         b_ps = banks("b_ps", "db")
@@ -232,10 +231,11 @@ def tile_picked_tfcdcrossbdifkmax_none_p_kernel(
             quantize(z2_q, z2_g, halves[h])
         for m in range(4):
             product(b_ps[m], x_cand, m, z2_q)
-        quantize(w3_q, w3_g)
+        for h in range(2):
+            nc.vector.quantize_mx(out=w3_q[0][:, halves[h]].bitcast(FP8X4), scales=w3_q[1][:, halves[h]], in_=w3_g[h][:])
         for h in range(2):
             for t in range(4):
-                n1_gather("sssvssss"[4 * h + t], t, h)
+                n1_gather("ssssssss"[4 * h + t], t, h)
         a_ps = banks("a_ps", "ya")
         for h in range(2):
             z_half(h)
@@ -243,19 +243,28 @@ def tile_picked_tfcdcrossbdifkmax_none_p_kernel(
         for m in range(4):
             product(a_ps[m], w3_q, m, z_q)
 
+        b_win[0] = new("b_win_held", [P, S + SPARE], F32, on="y_n1_0")
+        nc.gpsimd.memset(b_win[0][:, S:], 0.0)
+
         def list_halves(eng, dst, win, lst):
             if eng == "s":
                 gather("s", dst[:], win[:], lst[:])
             else:
                 for h in range(2):
-                    gather("v" if eng == "v" else "vs"[h], dst[:, halves[h]], win[:], lst[:, 16 * h : 16 * (h + 1)])
+                    gather({"v": "vv", "b": "vs", "h": "ss"}[eng][h], dst[:, halves[h]], win[:], lst[:, 16 * h : 16 * (h + 1)])
 
         for m in range(4):
-            scaled("ssss"[m], b_win[m][:, 0:S], b_ps[m][:], OUT_SCALE)
+            scaled("vsss"[m], b_win[m][:, 0:S], b_ps[m][:], OUT_SCALE)
             list_halves("ssss"[m], b_n5[m], b_win[m], n5_l)
         for m in range(4):
             cp("vvss"[m])(a_win[m][:, 0:S], a_ps[m][:])
-            list_halves("vvss"[m], a_n4[m], a_win[m], n4_l)
-            nc.vector.tensor_tensor(left[m][:], a_ps[m][:], b_n5[m][:], ALU.mult)
-            nc.vector.scalar_tensor_tensor(right[m][:], b_ps[m][:], OUT_SCALE, a_n4[m][:], ALU.mult, ALU.mult)
-            finish(m, nc.gpsimd if "gggv"[m] == "g" else nc.vector)
+            list_halves("vvsh"[m], a_n4[m], a_win[m], n4_l)
+            if "gvvv"[m] == "g":
+                nc.gpsimd.tensor_tensor(left[m][:], a_win[m][:, 0:S], b_n5[m][:], ALU.mult)
+            else:
+                nc.vector.tensor_tensor(left[m][:], a_ps[m][:], b_n5[m][:], ALU.mult)
+            for cols in (halves if m == 3 and 1 else [whole]):
+                nc.vector.scalar_tensor_tensor(right[m][:, cols], b_ps[m][:, cols], OUT_SCALE, a_n4[m][:, cols], ALU.mult, ALU.mult)
+            for cols in (halves if m == 3 and 1 else [whole]):
+                (nc.gpsimd if "gggv"[m] == "g" else nc.vector).tensor_tensor(res[m][:, cols], left[m][:, cols], right[m][:, cols], ALU.subtract)
+                nc.sync.dma_start(out[P * m : P * (m + 1), cols], res[m][:, cols])

@@ -2,8 +2,8 @@ from contextlib import ExitStack
 
 import concourse.mybir as mybir
 
-K, T, S, N, H, W, C = 512, 2048, 512, 512, 512, 384, 512
-FLOPS = 4 * 2 * 512 * 512 * 512
+K, T, S, W = 512, 2048, 512, 384
+FLOPS = 4 * 2 * K * S * S
 
 F32 = mybir.dt.float32
 BF16 = mybir.dt.bfloat16
@@ -17,7 +17,10 @@ COPY = mybir.ActivationFunctionType.Copy
 
 P = 128
 PACK = 4
-HALF = 256
+HALF = S // 2
+HALVES = [slice(0, HALF), slice(HALF, S)]
+WHOLE = slice(0, S)
+PER_COLUMN = 16
 SPARE = 32
 OUT_SCALE = 0.75 * 0.0625
 
@@ -29,242 +32,220 @@ def tile_picked_tfcdcrossbdifkmax_none_p_kernel(
     with ExitStack() as ctx:
         lists = ctx.enter_context(tc.tile_pool(name="lists", bufs=1))
         sb = ctx.enter_context(tc.tile_pool(name="sb", bufs=1))
+        w1_then_d = ctx.enter_context(tc.tile_pool(name="w1_then_d", bufs=1))
         ps = ctx.enter_context(tc.psum_pool(name="ps", bufs=1))
-        halves = [slice(0, HALF), slice(HALF, 2 * HALF)]
-        whole = slice(0, 512)
 
         def new(name, shape, dtype, on=None):
             return sb.tile(shape, dtype, name=name, tag=on or name, align_bytes=64)
 
-        def four(name, width, dtype=F32):
-            return [new("%s%d" % (name, t), [P, width], dtype) for t in range(4)]
+        def four(name, width):
+            return [new("%s%d" % (name, i), [P, width], F32) for i in range(PACK)]
 
-        def load_list(name, ap):
-            tl = lists.tile(list(ap.shape), U16, name=name)
-            nc.sync.dma_start(tl[:], ap)
+        def four_banks(name, tag):
+            return [ps.tile([P, S], F32, name="%s%d" % (name, i), tag="%s%d" % (tag, i)) for i in range(PACK)]
+
+        def mx_operand(name, words_on=None):
+            return new(name + "_words", [P, S], U32, words_on), new(name + "_scales", [P, S], U8)
+
+        def grouped_tile(name, on=None):
+            return new(name + "_grouped", [P, PACK * S], BF16, on)
+
+        def load_list(name, source):
+            tl = lists.tile(list(source.shape), U16, name=name)
+            nc.sync.dma_start(tl[:], source)
             return tl
 
-        def load_weight(name, w, cols):
-            raw = new(name, [P, PACK, cols.stop - cols.start], F32)
+        def load_weight(raw, w, cols):
             nc.sync.dma_start(raw[:], w.rearrange("(p j) c -> p j c", j=PACK)[:, :, cols])
             return raw
 
-        def load_gain(name, g):
+        def load_gain(name, gain):
             tl = new(name, [P, PACK], F32)
-            nc.sync.dma_start(tl[:], g.rearrange("(p t) o -> p (t o)", t=PACK))
+            nc.sync.dma_start(tl[:], gain.rearrange("(p t) o -> p (t o)", t=PACK))
             return tl
 
-        def codes(name, on=None):
-            return new(name + "_codes", [P, 512], U32, on)
+        def list_half(lst, h):
+            return lst[:, h * HALF // PER_COLUMN : (h + 1) * HALF // PER_COLUMN]
 
-        def scales(name, on=None):
-            return new(name + "_scales", [P, 512], U8, on)
-
-        def mx(name):
-            return (codes(name), scales(name))
-
-        def grouped(name, on=None):
-            return new(name + "_grouped", [P, 512 * PACK], BF16, on)
-
-        def pick_bytes(dst, lst):
-            nc.vector.tensor_copy(dst[:], xs[:].indirect(lst[:]))
-
-        def pick_words(dst, lst):
-            nc.vector.tensor_copy(dst[:], xw[:].bitcast(U32).indirect(lst[:]))
-
-        def words4(cols):
+        def grouped_cols(cols):
             return slice(PACK * cols.start, PACK * cols.stop)
 
-        def quantize(q, g, cols=whole):
-            nc.vector.quantize_mx(out=q[0][:, cols].bitcast(FP8X4), scales=q[1][:, cols], in_=g[:, words4(cols)])
+        def woven(grouped):
+            return grouped.rearrange("p (c i j) -> p c j i", i=4, j=PACK)
 
-        def product(bank, lhs, t, rhs, cols=whole):
-            st = slice(P * t, P * (t + 1))
-            nc.tensor.matmul_mx(
-                out=bank[:, cols], lhsT=lhs[0][:, st].bitcast(FP8X4), lhsT_scale=lhs[1][:, st],
-                rhs=rhs[0][:, cols].bitcast(FP8X4), rhs_scale=rhs[1][:, cols], start=True, stop=True,
+        def to_weave(rows):
+            return rows.rearrange("p j (c i) -> p c j i", i=4)
+
+        def deal_half(copy, grouped, raw, h):
+            rs = slice(h * HALF // PACK, (h + 1) * HALF // PACK)
+            copy(
+                grouped[:].rearrange("p (t r j) -> p r j t", t=PACK, j=PACK)[:, rs],
+                raw[:].rearrange("p j (r t) -> p r j t", t=PACK),
             )
 
-        def pool_cast(dst, src):
-            nc.gpsimd.tensor_scalar(dst, src, 1.0, 0.0, ALU.mult, ALU.add)
+        def quantize(operand, grouped, cols=WHOLE):
+            words, scales = operand
+            nc.vector.quantize_mx(
+                out=words[:, cols].bitcast(FP8X4), scales=scales[:, cols], in_=grouped[:, grouped_cols(cols)]
+            )
 
-        def cp(eng):
-            return {"s": nc.scalar.copy, "v": nc.vector.tensor_copy, "g": pool_cast}[eng]
+        def products(banks, stationary, moving):
+            for i, bank in enumerate(banks):
+                cols = slice(P * i, P * (i + 1))
+                nc.tensor.matmul_mx(
+                    out=bank[:],
+                    lhsT=stationary[0][:, cols].bitcast(FP8X4),
+                    lhsT_scale=stationary[1][:, cols],
+                    rhs=moving[0][:].bitcast(FP8X4),
+                    rhs_scale=moving[1][:],
+                    start=True,
+                    stop=True,
+                )
 
-        def deal_half(eng, g, raw, h):
-            dst = g[:].rearrange("p (t m j) -> p m j t", t=PACK, j=PACK)[:, 64 * h : 64 * (h + 1)]
-            cp(eng)(dst, raw[:].rearrange("p j (m t) -> p m j t", t=PACK))
+        def scalar_move(dst, src):
+            nc.scalar.activation(dst, src, COPY)
 
-        def weave_out(g):
-            return g.rearrange("p (c i t) -> p c t i", i=4, t=PACK)
-
-        def weave_in(planes):
-            return planes.rearrange("p t (c i) -> p c t i", i=4)
-
-        def weave(eng, g, planes, cols):
-            cp(eng)(weave_out(g[:, words4(cols)]), weave_in(planes[:, :, cols]))
-
-        def gather(eng, dst, win, lst):
-            if eng == "s":
-                nc.scalar.activation(dst, win.indirect(lst), COPY)
-            else:
-                nc.vector.tensor_copy(dst, win.indirect(lst))
-
-        def scatter(eng, win, lst, src):
-            if eng == "s":
-                nc.scalar.activation(win.indirect(lst), src, COPY)
-            else:
-                nc.vector.tensor_copy(win.indirect(lst), src)
-
-        def banks(name, tag):
-            return [ps.tile([P, S], F32, name="%s%d" % (name, t), tag="%s%d" % (tag, t)) for t in range(4)]
-
-        def scaled(eng, dst, src, scale):
-            if eng == "s":
-                nc.scalar.activation(dst, src, COPY, scale=scale)
-            elif eng == "g":
-                nc.gpsimd.tensor_scalar(dst, src, scale, 0.0, ALU.mult, ALU.add)
-            else:
-                nc.vector.tensor_scalar(dst, src, scale, None, ALU.mult)
-
-        def larger(t):
-            nc.vector.scalar_tensor_tensor(ra[t][:], old[t][:], 0.5, pa[t][:], ALU.mult, ALU.max)
-
-        def weigh(eng, t):
-            scaled(eng, z2_planes[:, t, :], d_win[t][:], gs_t[:, t : t + 1])
-
-        def y_out(eng, t):
-            scaled(eng, y_win[t][:], y_ps[t][:], gn_t[:, t : t + 1])
-            nc.sync.dma_start(y_all[:, t, :], y_win[t][:])
-
-        def n1_gather(eng, t, h):
-            gather(eng, y_n1[h][:, t, :], y_win[t][:], n1_l[:, 16 * h : 16 * (h + 1)])
-
-        def z_half(h):
-            cols = halves[h]
-            nc.vector.tensor_tensor(weave_out(z_g[:, words4(cols)]), weave_in(y_all[:, :, cols]), weave_in(y_n1[h][:]), ALU.subtract)
-
-        def finish(m, sub=nc.vector):
-            sub.tensor_tensor(res[m][:], left[m][:], right[m][:], ALU.subtract)
-            nc.sync.dma_start(out[P * m : P * (m + 1), :], res[m][:])
+        vector_move = nc.vector.tensor_copy
 
         xs = new("xs", [P, T], U8)
         nc.gpsimd.memset(xs[:].bitcast(I32), 0)
         two_l = load_list("two_l", two)
-        w2_raw = [load_weight("w2_raw0", w2, halves[0])]
         offs_l = load_list("offs_l", offs)
         for q in range(4):
             nc.sync.dma_start(xs[32 * q : 32 * q + 4, :].bitcast(I32), x_scales[0, 4 * q : 4 * q + 4, :].bitcast(I32))
-        w2_raw.append(load_weight("w2_raw1", w2, halves[1]))
+        w2_raw = [load_weight(new("w2_raw%d" % h, [P, PACK, HALF], F32), w2, HALVES[h]) for h in range(2)]
+        cand_l = load_list("cand_l", cand)
         xw = new("xw", [P, T], I32)
         nc.sync.dma_start(xw[:], x_words[0].rearrange("p c r -> p (c r)").bitcast(I32))
-        cand_l = load_list("cand_l", cand)
         n3_l = load_list("n3_l", n3)
         n2_l = load_list("n2_l", n2)
-        w1_raw = [load_weight("w1_raw%d" % h, w1, halves[h]) for h in range(2)]
+        half_bytes = PACK * HALF * 4
+        w1_raw = [
+            load_weight(w1_then_d.tile([P, PACK, HALF], F32, name="w1_raw%d" % h, offset=h * half_bytes), w1, HALVES[h])
+            for h in range(2)
+        ]
         gs_t = load_gain("gs_t", gs)
         gn_t = load_gain("gn_t", gn)
         n1_l = load_list("n1_l", n1)
-        w3_raw = load_weight("w3_raw", w3, whole)
+        w3_raw = load_weight(new("w3_raw", [P, PACK, S], F32), w3, WHOLE)
         n5_l = load_list("n5_l", n5)
         n4_l = load_list("n4_l", n4)
         a_win, b_win = four("a_win", S + SPARE), four("b_win", S + SPARE)
-        for win in a_win + b_win[1:]:
+        for win in a_win + b_win:
             nc.gpsimd.memset(win[:, S:], 0.0)
-        d_win = four("d_win", S)
-        pa, old, ra = [[new("%s%d" % (nm, u), [P, 2, W], F32) for u in range(2)] for nm in ("pa", "old", "ra")]
+
+        def pick_scales(operand, lst):
+            nc.vector.tensor_copy(operand[1][:], xs[:].indirect(lst[:]))
+
+        def pick_words(operand, lst):
+            nc.vector.tensor_copy(operand[0][:], xw[:].bitcast(U32).indirect(lst[:]))
+
+        old = new("old", [P, PACK, W], F32)
+        x_two, x_offs = mx_operand("x_two"), mx_operand("x_offs")
+        x_cand = mx_operand("x_cand", words_on="old")
+        w1_q, w2_q = mx_operand("w1"), mx_operand("w2")
+        w1_g, w2_g = grouped_tile("w1"), grouped_tile("w2")
+        pick_scales(x_two, two_l)
+        pick_scales(x_offs, offs_l)
+        pick_scales(x_cand, cand_l)
+        for h in range(2):
+            deal_half(nc.scalar.copy, w2_g, w2_raw[h], h)
+        quantize(w2_q, w2_g)
+        pick_words(x_two, two_l)
+        d_ps = four_banks("d_ps", "d_then_b")
+        products(d_ps, w2_q, x_two)
+        pick_words(x_offs, offs_l)
+        deal_half(nc.scalar.copy, w1_g, w1_raw[0], 0)
+        deal_half(nc.vector.tensor_copy, w1_g, w1_raw[1], 1)
+        quantize(w1_q, w1_g)
+        y_ps = four_banks("y_ps", "y_then_a")
+        products(y_ps, w1_q, x_offs)
+
         y_win = four("y_win", S)
         y_all = new("y_all", [P, PACK, S], F32)
-        y_n1 = [new("y_n1_%d" % h, [P, PACK, HALF], F32) for h in range(2)]
-        b_n5, a_n4, left, right, res = [four(nm, S) for nm in ("b_n5_", "a_n4_", "left", "right", "res")]
-        x_two, x_offs = mx("x_two"), mx("x_offs")
-        w1_q, w2_q, z_q, z2_q = [mx(nm) for nm in ("w1", "w2", "z", "z2")]
-        w1_g, w2_g, z2_g = [grouped(nm) for nm in ("w1", "w2", "z2")]
-        z_g = grouped("z", on="z2_grouped")
-        w3_g = [new("w3_g%d" % h, [P, HALF * PACK], BF16, on="pa%d" % h) for h in range(2)]
-        z2_planes = new("z2_planes", [P, PACK, S], BF16)
-        w3_q = (codes("w3", on="z2_planes"), scales("w3"))
-        x_cand = (codes("x_cand", on="old1"), scales("x_cand"))
 
-        pick_bytes(x_two[1], two_l)
-        pick_bytes(x_offs[1], offs_l)
-        deal_half("s", w2_g, w2_raw[0], 0)
-        deal_half("s", w2_g, w2_raw[1], 1)
-        quantize(w2_q, w2_g)
-        pick_words(x_two[0], two_l)
-        d_ps = banks("d_ps", "db")
-        for t in range(4):
-            product(d_ps[t], w2_q, t, x_two)
-        pick_words(x_offs[0], offs_l)
-        pick_bytes(x_cand[1], cand_l)
-        deal_half("g", w1_g, w1_raw[0], 0)
-        deal_half("g", w1_g, w1_raw[1], 1)
-        y_ps = banks("y_ps", "ya")
-        for u in range(2):
-            for e, eng in enumerate("vs"):
-                t = 2 * u + e
+        def y_out(t):
+            nc.scalar.activation(y_win[t][:], y_ps[t][:], COPY, scale=gn_t[:, t : t + 1])
+            nc.sync.dma_start(y_all[:, t, :], y_win[t][:])
+
+        d_win = [w1_then_d.tile([P, S], F32, name="d_win%d" % t, offset=t * S * 4) for t in range(PACK)]
+        pa = new("pa", [P, PACK, W], F32, on="w1_grouped")
+        for pair in range(2):
+            planes = (2 * pair, 2 * pair + 1)
+            both = slice(planes[0], planes[1] + 1)
+            for t in planes:
                 nc.scalar.copy(d_win[t][:], d_ps[t][:])
-            for e, eng in enumerate("vs"):
-                t = 2 * u + e
-                gather("vvssvvss"[2 * t], pa[u][:, e, :], d_win[t][:], n3_l[:])
-                gather("vvssvvss"[2 * t + 1], old[u][:, e, :], d_win[t][:], n2_l[:])
-            if u == 0:
-                quantize(w1_q, w1_g)
-                for t in range(4):
-                    product(y_ps[t], w1_q, t, x_offs)
-            larger(u)
-            if u == 1:
-                y_out("s", 0)
-                y_out("s", 1)
-            for e, eng in enumerate("vs"):
-                scatter(eng, d_win[2 * u + e][:], n2_l[:], ra[u][:, e, :])
-            cp("g")(weave_out(w3_g[u][:]), weave_in(w3_raw[:, :, halves[u]]))
-        pick_words(x_cand[0], cand_l)
-        for t in range(4):
-            weigh("vvvv"[t], t)
-        for t in range(2, 4):
-            y_out("s", t)
-        b_ps = banks("b_ps", "db")
-        for h in range(2):
-            weave("v", z2_g, z2_planes, halves[h])
-        for h in range(2):
-            quantize(z2_q, z2_g, halves[h])
-        for m in range(4):
-            product(b_ps[m], x_cand, m, z2_q)
-        for h in range(2):
-            nc.vector.quantize_mx(out=w3_q[0][:, halves[h]].bitcast(FP8X4), scales=w3_q[1][:, halves[h]], in_=w3_g[h][:])
-        for h in range(2):
-            for t in range(4):
-                n1_gather("ssssssss"[4 * h + t], t, h)
-        a_ps = banks("a_ps", "ya")
-        for h in range(2):
-            z_half(h)
-            quantize(z_q, z_g, halves[h])
-        for m in range(4):
-            product(a_ps[m], w3_q, m, z_q)
+            for t, own in zip(planes, (vector_move, scalar_move)):
+                by_n3, by_n2 = (vector_move, scalar_move) if pair == 0 else (own, own)
+                by_n3(pa[:, t, :], d_win[t][:].indirect(n3_l[:]))
+                by_n2(old[:, t, :], d_win[t][:].indirect(n2_l[:]))
+            ra = new("ra%d" % pair, [P, 2, W], F32)
+            nc.vector.scalar_tensor_tensor(ra[:], old[:, both, :], 0.5, pa[:, both, :], ALU.mult, ALU.max)
+            if pair == 1:
+                y_out(0)
+                y_out(1)
+            vector_move(d_win[planes[0]][:].indirect(n2_l[:]), ra[:, 0, :])
+            scalar_move(d_win[planes[1]][:].indirect(n2_l[:]), ra[:, 1, :])
 
-        b_win[0] = new("b_win_held", [P, S + SPARE], F32, on="y_n1_0")
-        nc.gpsimd.memset(b_win[0][:, S:], 0.0)
+        pick_words(x_cand, cand_l)
+        z2_rows = new("z2_rows", [P, PACK, S], BF16)
+        for t in range(PACK):
+            nc.vector.tensor_scalar(z2_rows[:, t, :], d_win[t][:], gs_t[:, t : t + 1], None, ALU.mult)
+        y_out(2)
+        y_out(3)
+        z2_g, z2_q = grouped_tile("z2"), mx_operand("z2")
+        for cols in HALVES:
+            nc.vector.tensor_copy(woven(z2_g[:, grouped_cols(cols)]), to_weave(z2_rows[:, :, cols]))
+        for cols in HALVES:
+            quantize(z2_q, z2_g, cols)
+        b_ps = four_banks("b_ps", "d_then_b")
+        products(b_ps, x_cand, z2_q)
 
-        def list_halves(eng, dst, win, lst):
-            if eng == "s":
-                gather("s", dst[:], win[:], lst[:])
+        w3_g, w3_q = grouped_tile("w3", on="z2_rows"), mx_operand("w3")
+        nc.vector.tensor_copy(woven(w3_g[:]), to_weave(w3_raw[:]))
+        quantize(w3_q, w3_g)
+        y_n1 = [new("y_n1_%d" % h, [P, PACK, HALF], F32) for h in range(2)]
+        for h in range(2):
+            for t in range(PACK):
+                scalar_move(y_n1[h][:, t, :], y_win[t][:].indirect(list_half(n1_l, h)))
+        z_g, z_q = grouped_tile("z", on="z2_grouped"), mx_operand("z")
+        for h, cols in enumerate(HALVES):
+            nc.vector.tensor_tensor(
+                woven(z_g[:, grouped_cols(cols)]), to_weave(y_all[:, :, cols]), to_weave(y_n1[h][:]), ALU.subtract
+            )
+            quantize(z_q, z_g, cols)
+        a_ps = four_banks("a_ps", "y_then_a")
+        products(a_ps, w3_q, z_q)
+
+        b_n5 = [new("b_n5_%d" % m, [P, S], F32, on="z2_grouped" if m == 1 else None) for m in range(PACK)]
+        for m in range(PACK):
+            nc.scalar.activation(b_win[m][:, WHOLE], b_ps[m][:], COPY, scale=OUT_SCALE)
+            if m == 1:
+                for h, cols in enumerate(HALVES):
+                    vector_move(b_n5[m][:, cols], b_win[m][:].indirect(list_half(n5_l, h)))
             else:
-                for h in range(2):
-                    gather({"v": "vv", "b": "vs", "h": "ss"}[eng][h], dst[:, halves[h]], win[:], lst[:, 16 * h : 16 * (h + 1)])
+                scalar_move(b_n5[m][:], b_win[m][:].indirect(n5_l[:]))
 
-        for m in range(4):
-            scaled("vsss"[m], b_win[m][:, 0:S], b_ps[m][:], OUT_SCALE)
-            list_halves("ssss"[m], b_n5[m], b_win[m], n5_l)
-        for m in range(4):
-            cp("vvss"[m])(a_win[m][:, 0:S], a_ps[m][:])
-            list_halves("vvsh"[m], a_n4[m], a_win[m], n4_l)
-            if "gvvv"[m] == "g":
-                nc.gpsimd.tensor_tensor(left[m][:], a_win[m][:, 0:S], b_n5[m][:], ALU.mult)
-            else:
+        left, right, res = four("left", S), four("right", S), four("res", S)
+        last = PACK - 1
+        for m in range(PACK):
+            pieces = HALVES if m == last else [WHOLE]
+            if m == 0:
+                nc.vector.tensor_copy(a_win[m][:, WHOLE], a_ps[m][:])
                 nc.vector.tensor_tensor(left[m][:], a_ps[m][:], b_n5[m][:], ALU.mult)
-            for cols in (halves if m == 3 and 1 else [whole]):
-                nc.vector.scalar_tensor_tensor(right[m][:, cols], b_ps[m][:, cols], OUT_SCALE, a_n4[m][:, cols], ALU.mult, ALU.mult)
-            for cols in (halves if m == 3 and 1 else [whole]):
-                (nc.gpsimd if "gggv"[m] == "g" else nc.vector).tensor_tensor(res[m][:, cols], left[m][:, cols], right[m][:, cols], ALU.subtract)
+                nc.vector.tensor_tensor(right[m][:], a_win[m][:].indirect(n4_l[:]), b_win[m][:, WHOLE], ALU.mult)
+            else:
+                a_n4 = new("a_n4_%d" % m, [P, S], F32)
+                nc.scalar.copy(a_win[m][:, WHOLE], a_ps[m][:])
+                for cols in pieces:
+                    entries = n4_l[:, cols.start // PER_COLUMN : cols.stop // PER_COLUMN]
+                    scalar_move(a_n4[:, cols], a_win[m][:].indirect(entries))
+                nc.vector.tensor_tensor(left[m][:], a_ps[m][:], b_n5[m][:], ALU.mult)
+                for cols in pieces:
+                    nc.vector.scalar_tensor_tensor(
+                        right[m][:, cols], b_ps[m][:, cols], OUT_SCALE, a_n4[:, cols], ALU.mult, ALU.mult
+                    )
+            subtracts = nc.gpsimd if m < 2 else nc.vector
+            for cols in pieces:
+                subtracts.tensor_tensor(res[m][:, cols], left[m][:, cols], right[m][:, cols], ALU.subtract)
                 nc.sync.dma_start(out[P * m : P * (m + 1), cols], res[m][:, cols])

from contextlib import ExitStack

import concourse.mybir as mybir

K, T, S, W = 512, 2048, 512, 384
FLOPS = 4 * 2 * K * S * S

F32 = mybir.dt.float32
BF16 = mybir.dt.bfloat16
I32 = mybir.dt.int32
U32 = mybir.dt.uint32
U16 = mybir.dt.uint16
U8 = mybir.dt.uint8
FP8X4 = mybir.dt.float8_e4m3fn_x4
ALU = mybir.AluOpType
COPY = mybir.ActivationFunctionType.Copy

P = 128
PACK = 4
HALF = S // 2
HALVES = [slice(0, HALF), slice(HALF, S)]
WHOLE = slice(0, S)
PER_COLUMN = 16
SPARE = 32
OUT_SCALE = 0.75 * 0.0625


def tile_picked_tfcdcrossbdifkmax_none_p_kernel(
    tc, x_words, x_scales, w1, w2, gn, w3, gs, offs, two, n1, n2, n3, cand, n4, n5, out
):
    nc = tc.nc
    with ExitStack() as ctx:
        lists = ctx.enter_context(tc.tile_pool(name="lists", bufs=1))
        sb = ctx.enter_context(tc.tile_pool(name="sb", bufs=1))
        w1_then_d = ctx.enter_context(tc.tile_pool(name="w1_then_d", bufs=1))
        ps = ctx.enter_context(tc.psum_pool(name="ps", bufs=1))

        def new(name, shape, dtype, on=None):
            return sb.tile(shape, dtype, name=name, tag=on or name, align_bytes=64)

        def four(name, width):
            return [new("%s%d" % (name, i), [P, width], F32) for i in range(PACK)]

        def four_banks(name, tag):
            return [ps.tile([P, S], F32, name="%s%d" % (name, i), tag="%s%d" % (tag, i)) for i in range(PACK)]

        def mx_operand(name, words_on=None):
            return new(name + "_words", [P, S], U32, words_on), new(name + "_scales", [P, S], U8)

        def grouped_tile(name, on=None):
            return new(name + "_grouped", [P, PACK * S], BF16, on)

        def load_list(name, source):
            tl = lists.tile(list(source.shape), U16, name=name)
            nc.sync.dma_start(tl[:], source)
            return tl

        def load_weight(raw, w, cols):
            nc.sync.dma_start(raw[:], w.rearrange("(p j) c -> p j c", j=PACK)[:, :, cols])
            return raw

        def load_gain(name, gain):
            tl = new(name, [P, PACK], F32)
            nc.sync.dma_start(tl[:], gain.rearrange("(p t) o -> p (t o)", t=PACK))
            return tl

        def list_half(lst, h):
            return lst[:, h * HALF // PER_COLUMN : (h + 1) * HALF // PER_COLUMN]

        def grouped_cols(cols):
            return slice(PACK * cols.start, PACK * cols.stop)

        def woven(grouped):
            return grouped.rearrange("p (c i j) -> p c j i", i=4, j=PACK)

        def to_weave(rows):
            return rows.rearrange("p j (c i) -> p c j i", i=4)

        def deal_half(copy, grouped, raw, h):
            rs = slice(h * HALF // PACK, (h + 1) * HALF // PACK)
            copy(
                grouped[:].rearrange("p (t r j) -> p r j t", t=PACK, j=PACK)[:, rs],
                raw[:].rearrange("p j (r t) -> p r j t", t=PACK),
            )

        def quantize(operand, grouped, cols=WHOLE):
            words, scales = operand
            nc.vector.quantize_mx(
                out=words[:, cols].bitcast(FP8X4), scales=scales[:, cols], in_=grouped[:, grouped_cols(cols)]
            )

        def products(banks, stationary, moving):
            for i, bank in enumerate(banks):
                cols = slice(P * i, P * (i + 1))
                nc.tensor.matmul_mx(
                    out=bank[:],
                    lhsT=stationary[0][:, cols].bitcast(FP8X4),
                    lhsT_scale=stationary[1][:, cols],
                    rhs=moving[0][:].bitcast(FP8X4),
                    rhs_scale=moving[1][:],
                    start=True,
                    stop=True,
                )

        def scalar_move(dst, src):
            nc.scalar.activation(dst, src, COPY)

        vector_move = nc.vector.tensor_copy

        xs = new("xs", [P, T], U8)
        nc.gpsimd.memset(xs[:].bitcast(I32), 0)
        two_l = load_list("two_l", two)
        offs_l = load_list("offs_l", offs)
        for q in range(4):
            nc.sync.dma_start(xs[32 * q : 32 * q + 4, :].bitcast(I32), x_scales[0, 4 * q : 4 * q + 4, :].bitcast(I32))
        w2_raw = [load_weight(new("w2_raw%d" % h, [P, PACK, HALF], F32), w2, HALVES[h]) for h in range(2)]
        cand_l = load_list("cand_l", cand)
        xw = new("xw", [P, T], I32)
        nc.sync.dma_start(xw[:], x_words[0].rearrange("p c r -> p (c r)").bitcast(I32))
        n3_l = load_list("n3_l", n3)
        n2_l = load_list("n2_l", n2)
        half_bytes = PACK * HALF * 4
        w1_raw = [
            load_weight(w1_then_d.tile([P, PACK, HALF], F32, name="w1_raw%d" % h, offset=h * half_bytes), w1, HALVES[h])
            for h in range(2)
        ]
        gs_t = load_gain("gs_t", gs)
        gn_t = load_gain("gn_t", gn)
        n1_l = load_list("n1_l", n1)
        w3_raw = load_weight(new("w3_raw", [P, PACK, S], F32), w3, WHOLE)
        n5_l = load_list("n5_l", n5)
        n4_l = load_list("n4_l", n4)
        a_win, b_win = four("a_win", S + SPARE), four("b_win", S + SPARE)
        for win in a_win + b_win:
            nc.gpsimd.memset(win[:, S:], 0.0)

        def pick_scales(operand, lst):
            nc.vector.tensor_copy(operand[1][:], xs[:].indirect(lst[:]))

        def pick_words(operand, lst):
            nc.vector.tensor_copy(operand[0][:], xw[:].bitcast(U32).indirect(lst[:]))

        old = new("old", [P, PACK, W], F32)
        x_two, x_offs = mx_operand("x_two"), mx_operand("x_offs")
        x_cand = mx_operand("x_cand", words_on="old")
        w1_q, w2_q = mx_operand("w1"), mx_operand("w2")
        w1_g, w2_g = grouped_tile("w1"), grouped_tile("w2")
        pick_scales(x_two, two_l)
        pick_scales(x_offs, offs_l)
        pick_scales(x_cand, cand_l)
        for h in range(2):
            deal_half(nc.scalar.copy, w2_g, w2_raw[h], h)
        quantize(w2_q, w2_g)
        pick_words(x_two, two_l)
        d_ps = four_banks("d_ps", "d_then_b")
        products(d_ps, w2_q, x_two)
        pick_words(x_offs, offs_l)
        deal_half(nc.scalar.copy, w1_g, w1_raw[0], 0)
        deal_half(nc.vector.tensor_copy, w1_g, w1_raw[1], 1)
        quantize(w1_q, w1_g)
        y_ps = four_banks("y_ps", "y_then_a")
        products(y_ps, w1_q, x_offs)

        y_win = four("y_win", S)
        y_all = new("y_all", [P, PACK, S], F32)

        def y_out(t):
            nc.scalar.activation(y_win[t][:], y_ps[t][:], COPY, scale=gn_t[:, t : t + 1])
            nc.sync.dma_start(y_all[:, t, :], y_win[t][:])

        d_win = [w1_then_d.tile([P, S], F32, name="d_win%d" % t, offset=t * S * 4) for t in range(PACK)]
        pa = new("pa", [P, PACK, W], F32, on="w1_grouped")
        for pair in range(2):
            planes = (2 * pair, 2 * pair + 1)
            both = slice(planes[0], planes[1] + 1)
            for t in planes:
                nc.scalar.copy(d_win[t][:], d_ps[t][:])
            for t, own in zip(planes, (vector_move, scalar_move)):
                by_n3, by_n2 = (vector_move, scalar_move) if pair == 0 else (own, own)
                by_n3(pa[:, t, :], d_win[t][:].indirect(n3_l[:]))
                by_n2(old[:, t, :], d_win[t][:].indirect(n2_l[:]))
            ra = new("ra%d" % pair, [P, 2, W], F32)
            nc.vector.scalar_tensor_tensor(ra[:], old[:, both, :], 0.5, pa[:, both, :], ALU.mult, ALU.max)
            if pair == 1:
                y_out(0)
                y_out(1)
            vector_move(d_win[planes[0]][:].indirect(n2_l[:]), ra[:, 0, :])
            scalar_move(d_win[planes[1]][:].indirect(n2_l[:]), ra[:, 1, :])

        pick_words(x_cand, cand_l)
        z2_rows = new("z2_rows", [P, PACK, S], BF16)
        for t in range(PACK):
            nc.vector.tensor_scalar(z2_rows[:, t, :], d_win[t][:], gs_t[:, t : t + 1], None, ALU.mult)
        y_out(2)
        y_out(3)
        z2_g, z2_q = grouped_tile("z2"), mx_operand("z2")
        for cols in HALVES:
            nc.vector.tensor_copy(woven(z2_g[:, grouped_cols(cols)]), to_weave(z2_rows[:, :, cols]))
        for cols in HALVES:
            quantize(z2_q, z2_g, cols)
        b_ps = four_banks("b_ps", "d_then_b")
        products(b_ps, x_cand, z2_q)

        w3_g, w3_q = grouped_tile("w3", on="z2_rows"), mx_operand("w3")
        nc.vector.tensor_copy(woven(w3_g[:]), to_weave(w3_raw[:]))
        quantize(w3_q, w3_g)
        y_n1 = [new("y_n1_%d" % h, [P, PACK, HALF], F32) for h in range(2)]
        for h in range(2):
            for t in range(PACK):
                scalar_move(y_n1[h][:, t, :], y_win[t][:].indirect(list_half(n1_l, h)))
        z_g, z_q = grouped_tile("z", on="z2_grouped"), mx_operand("z")
        for h, cols in enumerate(HALVES):
            nc.vector.tensor_tensor(
                woven(z_g[:, grouped_cols(cols)]), to_weave(y_all[:, :, cols]), to_weave(y_n1[h][:]), ALU.subtract
            )
            quantize(z_q, z_g, cols)
        a_ps = four_banks("a_ps", "y_then_a")
        products(a_ps, w3_q, z_q)

        b_n5 = [new("b_n5_%d" % m, [P, S], F32, on="z2_grouped" if m == 1 else None) for m in range(PACK)]
        for m in range(PACK):
            nc.scalar.activation(b_win[m][:, WHOLE], b_ps[m][:], COPY, scale=OUT_SCALE)
            if m == 1:
                for h, cols in enumerate(HALVES):
                    vector_move(b_n5[m][:, cols], b_win[m][:].indirect(list_half(n5_l, h)))
            else:
                scalar_move(b_n5[m][:], b_win[m][:].indirect(n5_l[:]))

        left, right, res = four("left", S), four("right", S), four("res", S)
        last = PACK - 1
        for m in range(PACK):
            pieces = HALVES if m == last else [WHOLE]
            if m == 0:
                nc.vector.tensor_copy(a_win[m][:, WHOLE], a_ps[m][:])
                nc.vector.tensor_tensor(left[m][:], a_ps[m][:], b_n5[m][:], ALU.mult)
                nc.vector.tensor_tensor(right[m][:], a_win[m][:].indirect(n4_l[:]), b_win[m][:, WHOLE], ALU.mult)
            else:
                a_n4 = new("a_n4_%d" % m, [P, S], F32)
                nc.scalar.copy(a_win[m][:, WHOLE], a_ps[m][:])
                for cols in pieces:
                    entries = n4_l[:, cols.start // PER_COLUMN : cols.stop // PER_COLUMN]
                    scalar_move(a_n4[:, cols], a_win[m][:].indirect(entries))
                nc.vector.tensor_tensor(left[m][:], a_ps[m][:], b_n5[m][:], ALU.mult)
                for cols in pieces:
                    nc.vector.scalar_tensor_tensor(
                        right[m][:, cols], b_ps[m][:, cols], OUT_SCALE, a_n4[:, cols], ALU.mult, ALU.mult
                    )
            subtracts = nc.gpsimd if m < 2 else nc.vector
            for cols in pieces:
                subtracts.tensor_tensor(res[m][:, cols], left[m][:, cols], right[m][:, cols], ALU.subtract)
                nc.sync.dma_start(out[P * m : P * (m + 1), cols], res[m][:, cols])
